import numpy as np
CORES = [0,1]
N = 2
ROOT = 0
def setup_inputs(rng):
    return {"x": rng.standard_normal((N, 128, 128), dtype=np.float32)}
def reference(x):
    y = np.full((N, 128, N * 128), np.nan, x.dtype)
    y[ROOT] = np.concatenate(list(x), axis=1)
    return {"y": y}

SCRATCH = {
    "stage": ("sbuf", [128, 128], "float32"),
    "land": ("sbuf", [128, 128], "float32"),
}
SEMAPHORES = ["loaded", "sent", "arrived", "own", "stored"]

W = 128


def rank_program(g, core, T, topo):
    rank = T.rank_of(core)
    if rank is None:
        return
    root = T.cores[0]

    if core != root:
        g.sync.dma_start(T.stage[:], T.x[:]).then_inc(T.sem.loaded, 16)
        g.wait_ge(T.sem.loaded, 16)
        rid, pid, _se = topo.addr(root)
        mask = topo.mask(core, root)
        g.remote_dma(T.land[:], T.stage[:], T.sem.arrived, T.sem.sent, pid, rid, mask)
        g.wait_ge(T.sem.sent, 16)
        return

    g.sync.dma_start(T.y[:, 0:W], T.x[:]).then_inc(T.sem.own, 16)
    g.scalar.wait_ge(T.sem.arrived, 16)
    g.scalar.dma_start(T.y[:, W:2 * W], T.land[:]).then_inc(T.sem.stored, 16)
    g.wait_ge(T.sem.own, 16)
    g.wait_ge(T.sem.stored, 16)
